import numpy as np
import ml_dtypes


def mxq(x, axis, fmt="e4m3"):
    dtype, down = {"e4m3": (ml_dtypes.float8_e4m3fn, 7), "e5m2": (ml_dtypes.float8_e5m2, 14)}[fmt]
    v = np.moveaxis(np.asarray(x, np.float32).astype(ml_dtypes.bfloat16).astype(np.float64), axis, -1)
    blocks = v.reshape(v.shape[:-1] + (-1, 32))
    amax = np.abs(blocks).max(-1, keepdims=True)
    byte = np.maximum(np.where(amax > 0, np.frexp(amax)[1] - 1 + 127, 0) - down, 1)
    scale = np.exp2(byte - 127.0)
    codes = (blocks / scale).astype(np.float32).astype(dtype).astype(np.float64)
    return np.moveaxis((codes * scale).reshape(v.shape), -1, axis)


WIDE = False


def mx_kscale(k):
    if not WIDE:
        return np.ones(k)
    levels = np.array([10, -10, 5, -5, 0])
    if k % 512:
        return np.exp2(np.random.permutation(np.resize(levels, k // 32))).repeat(32)
    a = np.empty((k // 512, 16))
    for p in range(k // 512):
        a[p, :8] = np.random.permutation(np.resize(levels, 8))
        for g in range(8):
            far = levels[np.abs(levels - a[p, g]) >= 10]
            a[p, g + 8] = far[np.random.randint(len(far))]
    return np.exp2(a.ravel()).repeat(32)


BF16 = ml_dtypes.bfloat16


def bf(x):
    return np.asarray(x, np.float32).astype(BF16)


def f64(x):
    return np.asarray(x).astype(np.float64)


E2M1 = np.array([0.0, 0.5, 1.0, 1.5, 2.0, 3.0, 4.0, 6.0, -0.0, -0.5, -1.0, -1.5, -2.0, -3.0, -4.0, -6.0])


def pack_weight(w, fmt):
    k, n = w.shape
    w = f64(bf(w)).reshape(k // 32, 32, n)
    amax = np.abs(w).max(1)
    if fmt == "e4m3":
        byte = np.frexp(amax)[1] - 1 + 127 - 7
    else:
        mant, ex = np.frexp(amax / 6.0)
        byte = np.where(mant > 0.5, ex, ex - 1) + 127
    byte = np.clip(np.where(amax > 0, byte, 1), 1, 254)
    scaled = (w * np.exp2(127.0 - byte)[:, None, :]).reshape(k, n).astype(np.float32)
    by_word = np.ascontiguousarray(scaled.reshape(k // 512, 128, 4, n).transpose(0, 1, 3, 2))
    if fmt == "e4m3":
        words = by_word.astype(ml_dtypes.float8_e4m3fn).view(np.uint8)
    else:
        c = by_word.astype(ml_dtypes.float4_e2m1fn).view(np.uint8) & 0xF
        words = c[..., 0::2] | (c[..., 1::2] << 4)
    return np.ascontiguousarray(words), np.ascontiguousarray(byte.astype(np.uint8).reshape(k // 512, 16, n))


def unpack_weight(words, scales, fmt):
    g, p, n, _ = words.shape
    if fmt == "e4m3":
        vals = np.ascontiguousarray(words).view(ml_dtypes.float8_e4m3fn).astype(np.float64)
    else:
        nib = np.empty((g, p, n, 4), np.uint8)
        nib[..., 0::2] = words & 0xF
        nib[..., 1::2] = words >> 4
        vals = E2M1[nib]
    vals = vals * np.repeat(np.exp2(scales.astype(np.float64) - 127.0), 8, axis=1)[..., None]
    return vals.transpose(0, 1, 3, 2).reshape(g * 512, n)
def pack4(w):
    words, scales = pack_weight(w, "e2m1")
    return words.reshape(words.shape[0], 128, -1), scales


def unpack4(words, scales):
    return unpack_weight(words.reshape(words.shape[0], 128, -1, 2), scales, "e2m1")


def planes(Y):
    n, m = Y.shape
    b = f64(bf(Y)).reshape(n // 32, 32, m)
    amax = np.abs(b).max(1)
    byte = np.clip(np.where(amax > 0, np.frexp(amax)[1] - 1 + 127 - 7, 1), 1, 254)
    codes = (b * np.exp2(127.0 - byte)[:, None, :]).reshape(n, m).astype(np.float32).astype(ml_dtypes.float8_e4m3fn).view(np.uint8)
    words = codes.reshape(n // 512, 128, 4, m).transpose(0, 1, 3, 2)
    return np.ascontiguousarray(words), np.ascontiguousarray(byte.astype(np.uint8).reshape(n // 512, 16, m))


G, S, T, DE, DK = 4, 1024, 512, 1536, 512

def setup_inputs():
    s = mx_kscale(G * DE)
    t = mx_kscale(G * DK).reshape(G, 1, DK)
    earlier_keys = np.random.randn(G, S, DE) * s.reshape(G, 1, DE)
    w = np.random.randn(G, DE, DK) / np.sqrt(DE) * t
    remap_words, remap_scales = pack4(w.reshape(G * DE, DK) / s[:, None])
    remap_bias = 0.3 * np.random.randn(G, DK) * t.reshape(G, DK)
    queries = 1.5 * np.random.randn(G, T, DK) / np.sqrt(DK) / t
    key_bias = 0.5 * np.random.randn(G, S)
    key_weight = np.exp(0.8 * np.random.randn(G, S))
    return {"earlier_keys": bf(earlier_keys), "remap_words": remap_words, "remap_scales": remap_scales,
            "remap_bias": bf(remap_bias), "queries": bf(queries),
            "key_bias": bf(key_bias), "key_weight": bf(key_weight)}

def reference(earlier_keys, remap_words, remap_scales, remap_bias, queries, key_bias, key_weight):
    W = unpack4(remap_words, remap_scales).reshape(G, DE, DK)
    keys = (mxq(f64(earlier_keys), 2) @ W) + f64(remap_bias)[:, None, :]
    scores = mxq(f64(queries), 2) @ mxq(keys, 2).swapaxes(1, 2)
    z = scores + f64(key_bias)[:, None, :]
    y = 1.0 / (1.0 + np.exp(-z)) * f64(key_weight)[:, None, :]
    Y = y.transpose(2, 0, 1).reshape(S, G * T)
    words, scales = planes(Y)
    return y, words, scales

@@ -1,0 +1,332 @@
+from contextlib import ExitStack
+
+import concourse.mybir as mybir
+from concourse.masks import make_identity
+
+G, S, T, DE, DK = 4, 1024, 512, 1536, 512
+FLOPS = 2 * G * S * DK * (DE + T)
+
+F32 = mybir.dt.float32
+BF16 = mybir.dt.bfloat16
+I32 = mybir.dt.int32
+U32 = mybir.dt.uint32
+U8 = mybir.dt.uint8
+FP8X4 = mybir.dt.float8_e4m3fn_x4
+FP4X4 = mybir.dt.float4_e2m1fn_x4
+ACT = mybir.ActivationFunctionType
+ALU = mybir.AluOpType
+
+P = 128
+PACK = 4
+K_PASS = P * PACK
+PASSES = DE // K_PASS
+HALVES = S // K_PASS
+UNITS = G * HALVES
+BANK = 512
+BANKS = 8
+R_ERAW, R_ESPLIT, R_STAGE, R_KROWS, R_Y, R_YOUT = 5, 3, 3, 3, 4, 8
+SMALL = G + 2 * UNITS
+PAIRS = 2 * UNITS
+TURNED = 2 * P * PACK
+K_LAG = 2
+FIRST_STEADY, LAST_STEADY = 4, 13
+ENG = {("KC", 15, 0): "dve", ("QP", 1, 0): "act", ("QC", 1, 0): "dve", ("PC", 3, 2): "act", ("QC", 0, 1): "dve", ("PC", 5, 2): "act", ("EC", 4, 1): "dve", ("EC", 3, 2): "dve", ("BC", 0, 1): "dve", ("YC", 6, 2): "dve", ("YC", 5, 1): "dve"}
+
+
+def copy_engine(kind, n, j):
+    return ENG.get((kind, n, j), "dve" if kind in ("PC", "QP") else "act")
+
+
+def steady_round(p):
+    unit, odd = divmod(p - 5, 2)
+    head, phase = divmod(p + 2, 4)
+    steps = [("KB", p - 1, 1), ("MQ", p, (4, 8))]
+    if phase in (1, 2):
+        steps += [("QT", head, phase - 1), ("QC", head, phase - 1)]
+    steps += [("ET", p + 1, 0), ("EC", p + 1, 0), ("YM", p - 3, 0), ("ET", p + 1, 1), ("EC", p + 1, 1)]
+    if not odd:
+        steps += [("YI", unit, 1)]
+    elif phase == 0:
+        steps += [("QP", head, 0)]
+    steps += [("YM", p - 3, 1), ("ET", p + 1, 2), ("EC", p + 1, 2), ("PC", p + 2, 2)]
+    if phase == 2:
+        steps += [("QQ", head, 0)]
+    for j in (2 * odd, 2 * odd + 1):
+        steps += [("YT", unit, j), ("YC", unit, j), ("SY", unit, j)]
+    steps += [("KT", p - 1, 2), ("KC", p - 1, 2), ("MQ", p + 1, (0, 4)), ("S1", p, 0)]
+    steps += [("YI", unit + 1, 0)] if odd else [("YQ", unit, 2), ("SW", unit, 0)]
+    steps += [("KB", p, 0), ("S1", p, 1)]
+    for j in range(2):
+        steps += [("S2", p - 2, j), ("SG", p - 2, j)]
+    steps += [("LE", p + 5, 2)]
+    if phase == 2:
+        steps += [("LW", head + 1, 0), ("LQ", head + 1, 0)]
+    return steps
+
+
+OPENING = [("LC", 0, 0), ("LE", 0, 0), ("LE", 0, 1), ("LW", 0, 0), ("LS", 0, 0), ("LE", 1, 0), ("LE", 1, 1), ("LE", 2, 2), ("LQ", 0, 0), ("LE", 3, 2), ("LE", 4, 2), ("ET", 0, 0), ("EC", 0, 0), ("ET", 0, 1), ("EC", 0, 1), ("MQ", 0, (0, 2)), ("MQ", 0, (2, 4)), ("CT", 0, 0), ("ET", 0, 2), ("CC", 0, 0), ("EC", 0, 2), ("BT", 0, 0), ("BC", 0, 0), ("PC", 1, 0), ("MQ", 0, (4, 6)), ("PC", 1, 1), ("S1", 0, 0), ("ET", 1, 1), ("ET", 1, 0), ("EC", 1, 1), ("EC", 1, 0), ("ET", 1, 2), ("EC", 1, 2), ("LE", 5, 2), ("BT", 0, 1), ("PC", 2, 2), ("KB", 0, 0), ("QP", 0, 0), ("MQ", 1, (0, 4)), ("BC", 0, 1), ("MQ", 1, (4, 6)), ("ET", 2, 0), ("QT", 0, 1), ("QT", 0, 0), ("QC", 0, 1), ("EC", 2, 0), ("ET", 2, 1), ("EC", 2, 1), ("ET", 2, 2), ("S1", 0, 1), ("KB", 0, 1), ("S1", 1, 0), ("S1", 1, 1), ("KT", 0, 2), ("EC", 2, 2), ("KB", 1, 0), ("PC", 3, 2), ("QC", 0, 0), ("KC", 0, 2), ("MQ", 2, (0, 4)), ("LE", 6, 2), ("LQ", 1, 0), ("LS", 1, 0), ("LW", 1, 0), ("KB", 1, 1), ("QQ", 0, 0), ("MQ", 2, (4, 8)), ("ET", 3, 0), ("EC", 3, 0), ("ET", 3, 1), ("EC", 3, 1), ("ET", 3, 2), ("EC", 3, 2), ("PC", 4, 2), ("KT", 1, 2), ("KC", 1, 2), ("QP", 1, 0), ("MQ", 3, (0, 4)), ("S1", 2, 0), ("KB", 2, 0), ("S2", 0, 0), ("S1", 2, 1), ("SG", 0, 0), ("S2", 0, 1), ("SG", 0, 1), ("LE", 7, 2), ("KB", 2, 1), ("MQ", 3, (4, 8)), ("YM", 0, 0), ("YM", 0, 1), ("ET", 4, 2), ("QT", 1, 0), ("QC", 1, 0), ("ET", 4, 0), ("ET", 4, 1), ("EC", 4, 1), ("EC", 4, 2), ("EC", 4, 0), ("PC", 5, 2), ("KT", 2, 2), ("KC", 2, 2), ("S1", 3, 0), ("KB", 3, 0), ("MQ", 4, (0, 4)), ("S2", 1, 0), ("S1", 3, 1), ("SG", 1, 0), ("S2", 1, 1), ("SG", 1, 1), ("LE", 8, 2)]
+CLOSING = [("KB", 13, 1), ("MQ", 14, (4, 8)), ("ET", 15, 0), ("EC", 15, 0), ("YM", 11, 0), ("ET", 15, 1), ("EC", 15, 1), ("YM", 11, 1), ("ET", 15, 2), ("EC", 15, 2), ("YT", 4, 2), ("YC", 4, 2), ("SY", 4, 2), ("YT", 4, 3), ("YC", 4, 3), ("SY", 4, 3), ("S1", 14, 0), ("YI", 5, 0), ("MQ", 15, (0, 4)), ("KB", 14, 0), ("S1", 14, 1), ("S2", 12, 0), ("SG", 12, 0), ("S2", 12, 1), ("KT", 13, 2), ("KC", 13, 2), ("SG", 12, 1), ("KB", 14, 1), ("YT", 5, 0), ("YC", 5, 0), ("SY", 5, 0), ("YI", 5, 1), ("MQ", 15, (4, 8)), ("YT", 5, 1), ("YC", 5, 1), ("SY", 5, 1), ("KT", 14, 2), ("KC", 14, 2), ("YT", 5, 2), ("YC", 5, 2), ("SY", 5, 2), ("YT", 5, 3), ("YC", 5, 3), ("SY", 5, 3), ("YQ", 5, 2), ("SW", 5, 0), ("SS", 0, 0), ("MQ", 16, (6, 8)), ("S1", 15, 0), ("KB", 15, 0), ("S1", 15, 1), ("S2", 13, 0), ("SG", 13, 0), ("S2", 13, 1), ("SG", 13, 1), ("S2", 14, 0), ("KT", 15, 0), ("KB", 15, 1), ("YM", 12, 0), ("YM", 12, 1), ("KC", 15, 0), ("KT", 15, 1), ("S2", 14, 1), ("YM", 13, 0), ("MQ", 17, (6, 7)), ("KC", 15, 1), ("SG", 14, 0), ("SG", 14, 1), ("YM", 13, 1), ("MQ", 17, (7, 8)), ("S2", 15, 0), ("SG", 15, 0), ("S2", 15, 1), ("SG", 15, 1), ("YI", 6, 0), ("YM", 14, 0), ("YM", 14, 1), ("YI", 6, 1), ("YT", 6, 0), ("YC", 6, 0), ("SY", 6, 0), ("YT", 6, 1), ("YC", 6, 1), ("SY", 6, 1), ("YT", 6, 2), ("YT", 6, 3), ("YM", 15, 0), ("YM", 15, 1), ("YC", 6, 2), ("SY", 6, 2), ("YQ", 6, 2), ("SW", 6, 0), ("YC", 6, 3), ("SY", 6, 3), ("YT", 7, 0), ("YC", 7, 0), ("SY", 7, 0), ("YT", 7, 1), ("YC", 7, 1), ("SY", 7, 1), ("YI", 7, 0), ("YI", 7, 1), ("YQ", 7, 0), ("YQ", 7, 1), ("SW", 7, 0), ("YT", 7, 2), ("YC", 7, 2), ("SY", 7, 2), ("YT", 7, 3), ("YC", 7, 3), ("SY", 7, 3), ("SS", 1, 0)]
+LIMIT = {"LE": 16, "PC": 16, "ET": 16, "EC": 16, "S1": 16, "KB": 16, "KT": 16, "KC": 16, "S2": 16, "SG": 16, "YM": 16, "MQ": 18,
+         "YI": 8, "YQ": 8, "SW": 8, "YT": 8, "YC": 8, "SY": 8, "LW": 4, "LQ": 4, "QP": 4, "QT": 4, "QC": 4, "QQ": 4}
+
+
+def schedule():
+    steps = list(OPENING)
+    for p in range(FIRST_STEADY, LAST_STEADY + 1):
+        steps += [s for s in steady_round(p) if 0 <= s[1] < LIMIT[s[0]]]
+    return steps + list(CLOSING)
+
+
+def tile_cross_layer_key_scores_k7_kernel(
+    tc, earlier_keys, remap_words, remap_scales, remap_bias, queries, key_bias, key_weight, out_0, out_1, out_2
+):
+    nc = tc.nc
+    with ExitStack() as ctx:
+        sb = ctx.enter_context(tc.tile_pool(name="sb", bufs=1))
+        ps = ctx.enter_context(tc.psum_pool(name="ps", bufs=1))
+
+        def ring(label, count, shape, dtype):
+            return [sb.tile(shape, dtype, name="%s%d" % (label, i), align_bytes=64) for i in range(count)]
+
+        banks = [ps.tile([P, BANK], F32, name="bank%d" % i) for i in range(BANKS)]
+        ident = sb.tile([P, P], F32, name="ident", align_bytes=64)
+        w_codes = sb.tile([P, G * PASSES, 2 * DK], U8, name="w_codes", align_bytes=64)
+        w_scales = sb.tile([P, G * PASSES, DK], U8, name="w_scales", align_bytes=64)
+        small_rows = sb.tile([P, K_PASS], BF16, name="small_rows", align_bytes=64)
+        small_cols = sb.tile([P, SMALL, PACK], BF16, name="small_cols", align_bytes=64)
+        bias_rows = sb.tile([P, G, DK], BF16, name="bias_rows", align_bytes=64)
+        warm = sb.tile([P, 1], F32, name="warm", align_bytes=64)
+        y_scales = sb.tile([P, HALVES, G * T], U8, name="y_scales", align_bytes=64)
+        q_codes = sb.tile([P, G, T], U32, name="q_codes", align_bytes=64)
+        q_scales = sb.tile([P, G, T], U8, name="q_scales", align_bytes=64)
+        q_split = sb.tile([P, 2, PACK * P], F32, name="q_split", align_bytes=64)
+        q_t = sb.tile([P, 2 * TURNED], BF16, name="q_t", align_bytes=64)
+        y_bf = sb.tile([P, T, PACK], BF16, name="y_bf", align_bytes=64)
+        e_raw = ring("e_raw", R_ERAW, [P, 2, DE], BF16)
+        e_split = ring("e_split", R_ESPLIT, [P, 2, 2 * PASSES * P], F32)
+        stage = ring("stage", R_STAGE, [P, 4 * TURNED], BF16)
+        codes = ring("codes", R_STAGE, [P, TURNED], U32)
+        scales = ring("scales", R_STAGE, [P, TURNED], U8)
+        q_raw = ring("q_raw", 2, [P, PACK, DK], BF16)
+        k_rows = ring("k_rows", R_KROWS, [P, 2, DK], BF16)
+        y_st = ring("y_st", R_Y, [P, PACK, T], F32)
+        y_codes = ring("y_codes", 2, [P, T], U32)
+        y_out = ring("y_out", R_YOUT, [P, K_PASS], F32)
+
+        ctx.enter_context(tc.manual_schedule())
+
+        nc.vector.memset(warm[:], 0.0)
+        nc.vector.memset(small_rows[:].bitcast(I32), 0)
+        nc.vector.memset(w_scales[:, :PASSES, :].rearrange("p g n -> p (g n)").bitcast(I32), 0)
+        nc.vector.memset(w_scales[:, PASSES:, :].rearrange("p g n -> p (g n)").bitcast(I32), 0)
+        make_identity(nc, ident[:])
+        nc.scalar.activation(out=warm[:], in_=warm[:], func=ACT.Sigmoid)
+
+        held = {}
+        used = []
+
+        def take_bank(kind, n, j):
+            bank = banks[len(used) % BANKS]
+            used.append(kind)
+            held[(kind, n, j)] = bank
+            return bank
+
+        def turn_words(bank, blocks):
+            for i, block in enumerate(blocks):
+                nc.tensor.transpose(bank[:, i * P : (i + 1) * P], block, ident[:])
+
+        def join_words(eng, dst, bank):
+            out = dst.bitcast(F32).rearrange("p (j r u) -> p j r u", r=P, u=2)
+            src = bank[:, : out.shape[1] * 2 * P].rearrange("p (j u r) -> p j r u", r=P, u=2)
+            if eng == "act":
+                nc.scalar.copy(out=out, in_=src)
+            else:
+                nc.vector.tensor_copy(out=out, in_=src)
+
+        def quantize(words, scale_bytes, src):
+            nc.vector.quantize_mx(out=words.bitcast(FP8X4), scales=scale_bytes, in_=src)
+
+        def copy_on(eng, out, src):
+            if eng == "act":
+                nc.scalar.copy(out=out, in_=src)
+            else:
+                nc.vector.tensor_copy(out=out, in_=src)
+
+        for kind, n, j in schedule():
+            h, g = divmod(n, HALVES)
+            unit, hf = divmod(n, 2)
+            slots = slice(0, 2) if j == 2 else slice(j, j + 1) if kind in ("LE", "PC", "YQ", "KT", "KC") else None
+            if kind == "LE":
+                head, half = divmod(unit, HALVES)
+                rows = earlier_keys[head, half * K_PASS : (half + 1) * K_PASS, :].rearrange("(p t) k -> p t k", t=PACK)
+                nc.sync.dma_start(out=e_raw[n % R_ERAW][:, slots, :], in_=rows[:, 2 * hf + slots.start : 2 * hf + slots.stop, :])
+            elif kind == "LQ":
+                nc.sync.dma_start(out=q_raw[n % 2][:], in_=queries[n].rearrange("(b r) k -> r b k", r=P))
+            elif kind == "LW":
+                nc.sync.dma_start(
+                    out=w_codes[:, PASSES * n : PASSES * (n + 1), :].bitcast(I32),
+                    in_=remap_words.bitcast(I32)[PASSES * n : PASSES * (n + 1), :, :].rearrange("g p n -> p g n"),
+                )
+            elif kind == "LC":
+                nc.gpsimd.dma_start(out=small_rows[0:G, :], in_=remap_bias)
+                nc.gpsimd.dma_start(
+                    out=small_rows[G : G + UNITS, :], in_=key_bias.rearrange("h (g s) -> (h g) s", g=HALVES)
+                )
+                nc.gpsimd.dma_start(
+                    out=small_rows[G + UNITS : SMALL, :], in_=key_weight.rearrange("h (g s) -> (h g) s", g=HALVES)
+                )
+            elif kind == "LS":
+                groups = slice(0, PASSES) if n == 0 else slice(PASSES, G * PASSES)
+                for quad in range(4):
+                    nc.sync.dma_start(
+                        out=w_scales[32 * quad : 32 * quad + 4, groups, :].bitcast(I32),
+                        in_=remap_scales.bitcast(I32)[groups, 4 * quad : 4 * quad + 4, :].rearrange("g r n -> r g n"),
+                    )
+            elif kind == "CT":
+                words = small_rows[:].bitcast(F32)
+                turn_words(take_bank(kind, n, j), [words[:, u : 2 * P : 2] for u in range(2)])
+            elif kind == "CC":
+                nc.scalar.copy(
+                    out=small_cols[:].bitcast(F32),
+                    in_=held[("CT", n, j)][:, : 2 * P].rearrange("p (u r) -> p r u", u=2)[:, :SMALL, :],
+                )
+            elif kind == "PC":
+                cols = slice(slots.start * PASSES * P, slots.stop * PASSES * P)
+                words = e_raw[n % R_ERAW][:, slots, :].rearrange("p t k -> p (t k)").bitcast(F32)
+                copy_on(copy_engine(kind, n, j), e_split[n % R_ESPLIT][:, :, cols], words.rearrange("p (m u) -> p u m", u=2))
+            elif kind == "QP":
+                words = q_raw[n % 2][:].rearrange("p b k -> p (b k)").bitcast(F32)
+                copy_on(copy_engine(kind, n, j), q_split[:], words.rearrange("p (m u) -> p u m", u=2))
+            elif kind == "ET":
+                blocks = []
+                for jj in (2 * j, 2 * j + 1):
+                    t, c = divmod(jj, PASSES)
+                    for u in range(2):
+                        if n > 0:
+                            blocks.append(e_split[n % R_ESPLIT][:, u, jj * P : (jj + 1) * P])
+                        else:
+                            words = e_raw[n % R_ERAW][:, t, :].bitcast(F32)
+                            blocks.append(words[:, 2 * P * c + u : 2 * P * (c + 1) : 2])
+                turn_words(take_bank(kind, n, j), blocks)
+            elif kind == "EC":
+                join_words(copy_engine(kind, n, j), stage[n % R_STAGE][:, j * TURNED : (j + 1) * TURNED], held[("ET", n, j)])
+            elif kind == "MQ":
+                cols = slice(P * j[0], P * j[1])
+                quantize(
+                    codes[n % R_STAGE][:, cols],
+                    scales[n % R_STAGE][:, cols],
+                    stage[n % R_STAGE][:, j[0] * K_PASS : j[1] * K_PASS],
+                )
+            elif kind == "S1":
+                bank = take_bank(kind, n, j)
+                for c in range(PASSES):
+                    cols = slice((PASSES * j + c) * P, (PASSES * j + c + 1) * P)
+                    nc.tensor.matmul_mx(
+                        out=bank[:],
+                        lhsT=codes[n % R_STAGE][:, cols].bitcast(FP8X4),
+                        lhsT_scale=scales[n % R_STAGE][:, cols],
+                        rhs=w_codes[:, PASSES * (n // 4) + c, :].bitcast(FP4X4),
+                        rhs_scale=w_scales[:, PASSES * (n // 4) + c, :],
+                        start=(c == 0),
+                        stop=(c == PASSES - 1),
+                    )
+            elif kind == "KB":
+                nc.vector.tensor_tensor(
+                    out=k_rows[n % R_KROWS][:, j, :].rearrange("p (u m e) -> p u m e", u=2, e=2),
+                    in0=held[("S1", n, j)][:].rearrange("p (m u e) -> p u m e", u=2, e=2),
+                    in1=bias_rows[:, n // 4, :].rearrange("p (u m e) -> p u m e", u=2, e=2),
+                    op=ALU.add,
+                )
+            elif kind == "KT":
+                blocks = []
+                for t in range(slots.start, slots.stop):
+                    words = k_rows[n % R_KROWS][:, t, :].bitcast(F32)
+                    for u in range(2):
+                        blocks.append(words[:, u * P : (u + 1) * P])
+                turn_words(take_bank(kind, n, j), blocks)
+            elif kind == "KC":
+                join_words(copy_engine(kind, n, j), stage[(n + K_LAG) % R_STAGE][:, (6 + slots.start) * K_PASS : (6 + slots.stop) * K_PASS], held[("KT", n, j)])
+            elif kind == "QT":
+                blocks = []
+                for b in (2 * j, 2 * j + 1):
+                    for u in range(2):
+                        blocks.append(q_split[:, u, b * P : (b + 1) * P])
+                turn_words(take_bank(kind, n, j), blocks)
+            elif kind == "QC":
+                join_words(copy_engine(kind, n, j), q_t[:, j * TURNED : (j + 1) * TURNED], held[("QT", n, j)])
+            elif kind == "QQ":
+                quantize(q_codes[:, n, :], q_scales[:, n, :], q_t[:])
+            elif kind == "S2":
+                cols = slice((6 + j) * P, (7 + j) * P)
+                nc.tensor.matmul_mx(
+                    out=take_bank(kind, n, j)[:],
+                    lhsT=codes[(n + K_LAG) % R_STAGE][:, cols].bitcast(FP8X4),
+                    lhsT_scale=scales[(n + K_LAG) % R_STAGE][:, cols],
+                    rhs=q_codes[:, n // 4, :].bitcast(FP8X4),
+                    rhs_scale=q_scales[:, n // 4, :],
+                    start=True,
+                    stop=True,
+                )
+            elif kind == "SG":
+                t = 2 * hf + j
+                nc.scalar.activation(
+                    out=y_st[unit % R_Y][:, t, :],
+                    in_=held[("S2", n, j)][:],
+                    func=ACT.Sigmoid,
+                    bias=small_cols[:, G + unit, t : t + 1],
+                )
+            elif kind == "YM":
+                t = 2 * hf + j
+                nc.vector.tensor_scalar(
+                    out=y_st[unit % R_Y][:, t, :],
+                    in0=y_st[unit % R_Y][:, t, :],
+                    scalar1=small_cols[:, G + UNITS + unit, t : t + 1],
+                    scalar2=None,
+                    op0=ALU.mult,
+                )
+            elif kind == "YI":
+                cols = slice(j * T // 2, (j + 1) * T // 2)
+                nc.vector.tensor_copy(
+                    out=y_bf[:, cols, :].rearrange("p (c i) t -> p c t i", i=PACK),
+                    in_=y_st[n % R_Y][:, :, cols].rearrange("p t (c i) -> p c t i", i=PACK),
+                )
+            elif kind == "YQ":
+                cols = slice(slots.start * T // 2, slots.stop * T // 2)
+                quantize(
+                    y_codes[n % 2][:, cols],
+                    y_scales[:, g, h * T + cols.start : h * T + cols.stop],
+                    y_bf[:, cols, :].rearrange("p c t -> p (c t)"),
+                )
+            elif kind == "SW":
+                words = out_1[g].rearrange("p m t -> p (m t)").bitcast(I32)
+                nc.sync.dma_start(out=words[:, h * T : (h + 1) * T], in_=y_codes[n % 2][:].bitcast(I32))
+            elif kind == "SS":
+                cols = slice(0, (G - 1) * T // 4) if n == 0 else slice((G - 1) * T // 4, G * T // 4)
+                for quad in range(4):
+                    queue = nc.scalar if n == 1 and quad % 2 else nc.sync
+                    queue.dma_start(
+                        out=out_2.bitcast(I32)[:, 4 * quad : 4 * quad + 4, cols].rearrange("g r m -> r g m"),
+                        in_=y_scales[32 * quad : 32 * quad + 4, :, :].bitcast(I32)[:, :, cols],
+                    )
+            elif kind == "YT":
+                turn_words(take_bank(kind, n, j), [y_st[n % R_Y][:, t, j * P : (j + 1) * P] for t in range(PACK)])
+            elif kind == "YC":
+                copy_on(
+                    copy_engine(kind, n, j),
+                    y_out[(PACK * n + j) % R_YOUT][:].rearrange("r (p t) -> r p t", t=PACK),
+                    held[("YT", n, j)][:].rearrange("r (t p) -> r p t", t=PACK),
+                )
+            elif kind == "SY":
+                nc.sync.dma_start(
+                    out=out_0[h, j * P : (j + 1) * P, g * K_PASS : (g + 1) * K_PASS], in_=y_out[(PACK * n + j) % R_YOUT][:]
+                )
+            elif kind == "BT":
+                words = small_cols[:].bitcast(F32)
+                blocks = [words[:, hh, u : u + 1].to_broadcast([P, P]) for hh in (2 * j, 2 * j + 1) for u in range(2)]
+                turn_words(take_bank(kind, n, j), blocks)
+            elif kind == "BC":
+                copy_on(
+                    copy_engine(kind, n, j),
+                    bias_rows[:, 2 * j : 2 * j + 2, :].rearrange("p h k -> p (h k)").bitcast(F32),
+                    held[("BT", n, j)][:],
+                )

@@ -13,8 +13,6 @@ U32 = mybir.dt.uint32
 U8 = mybir.dt.uint8
 FP8X4 = mybir.dt.float8_e4m3fn_x4
 FP4X4 = mybir.dt.float4_e2m1fn_x4
-ACT = mybir.ActivationFunctionType
-ALU = mybir.AluOpType
 
 P = 128
 PACK = 4
@@ -22,59 +20,26 @@ K_PASS = P * PACK
 PASSES = DE // K_PASS
 HALVES = S // K_PASS
 UNITS = G * HALVES
-BANK = 512
-BANKS = 8
-R_ERAW, R_ESPLIT, R_STAGE, R_KROWS, R_Y, R_YOUT = 5, 3, 3, 3, 4, 8
-SMALL = G + 2 * UNITS
 PAIRS = 2 * UNITS
-TURNED = 2 * P * PACK
-K_LAG = 2
-FIRST_STEADY, LAST_STEADY = 4, 13
-ENG = {("KC", 15, 0): "dve", ("QP", 1, 0): "act", ("QC", 1, 0): "dve", ("PC", 3, 2): "act", ("QC", 0, 1): "dve", ("PC", 5, 2): "act", ("EC", 4, 1): "dve", ("EC", 3, 2): "dve", ("BC", 0, 1): "dve", ("YC", 6, 2): "dve", ("YC", 5, 1): "dve"}
+PAIRS_PER_HEAD = PAIRS // G
+BANKS = 8
+BOTH = (0, 2)
+
+E_BLOCKS = 2 * PASSES
+BLOCKS = E_BLOCKS + 2
+K_LAG = 3
+
+ROW_KEY_BIAS = G
+ROW_KEY_WEIGHT = G + UNITS
+SMALL_ROWS = G + 2 * UNITS
+
+RAW_RING, SPLIT_RING, STAGE_RING, KEYS_RING, Y_RING, OUT_RING = 5, 3, 3, 3, 4, 4
 
 
-def copy_engine(kind, n, j):
-    return ENG.get((kind, n, j), "dve" if kind in ("PC", "QP") else "act")
-
-
-def steady_round(p):
-    unit, odd = divmod(p - 5, 2)
-    head, phase = divmod(p + 2, 4)
-    steps = [("KB", p - 1, 1), ("MQ", p, (4, 8))]
-    if phase in (1, 2):
-        steps += [("QT", head, phase - 1), ("QC", head, phase - 1)]
-    steps += [("ET", p + 1, 0), ("EC", p + 1, 0), ("YM", p - 3, 0), ("ET", p + 1, 1), ("EC", p + 1, 1)]
-    if not odd:
-        steps += [("YI", unit, 1)]
-    elif phase == 0:
-        steps += [("QP", head, 0)]
-    steps += [("YM", p - 3, 1), ("ET", p + 1, 2), ("EC", p + 1, 2), ("PC", p + 2, 2)]
-    if phase == 2:
-        steps += [("QQ", head, 0)]
-    for j in (2 * odd, 2 * odd + 1):
-        steps += [("YT", unit, j), ("YC", unit, j), ("SY", unit, j)]
-    steps += [("KT", p - 1, 2), ("KC", p - 1, 2), ("MQ", p + 1, (0, 4)), ("S1", p, 0)]
-    steps += [("YI", unit + 1, 0)] if odd else [("YQ", unit, 2), ("SW", unit, 0)]
-    steps += [("KB", p, 0), ("S1", p, 1)]
-    for j in range(2):
-        steps += [("S2", p - 2, j), ("SG", p - 2, j)]
-    steps += [("LE", p + 5, 2)]
-    if phase == 2:
-        steps += [("LW", head + 1, 0), ("LQ", head + 1, 0)]
-    return steps
-
-
-OPENING = [("LC", 0, 0), ("LE", 0, 0), ("LE", 0, 1), ("LW", 0, 0), ("LS", 0, 0), ("LE", 1, 0), ("LE", 1, 1), ("LE", 2, 2), ("LQ", 0, 0), ("LE", 3, 2), ("LE", 4, 2), ("ET", 0, 0), ("EC", 0, 0), ("ET", 0, 1), ("EC", 0, 1), ("MQ", 0, (0, 2)), ("MQ", 0, (2, 4)), ("CT", 0, 0), ("ET", 0, 2), ("CC", 0, 0), ("EC", 0, 2), ("BT", 0, 0), ("BC", 0, 0), ("PC", 1, 0), ("MQ", 0, (4, 6)), ("PC", 1, 1), ("S1", 0, 0), ("ET", 1, 1), ("ET", 1, 0), ("EC", 1, 1), ("EC", 1, 0), ("ET", 1, 2), ("EC", 1, 2), ("LE", 5, 2), ("BT", 0, 1), ("PC", 2, 2), ("KB", 0, 0), ("QP", 0, 0), ("MQ", 1, (0, 4)), ("BC", 0, 1), ("MQ", 1, (4, 6)), ("ET", 2, 0), ("QT", 0, 1), ("QT", 0, 0), ("QC", 0, 1), ("EC", 2, 0), ("ET", 2, 1), ("EC", 2, 1), ("ET", 2, 2), ("S1", 0, 1), ("KB", 0, 1), ("S1", 1, 0), ("S1", 1, 1), ("KT", 0, 2), ("EC", 2, 2), ("KB", 1, 0), ("PC", 3, 2), ("QC", 0, 0), ("KC", 0, 2), ("MQ", 2, (0, 4)), ("LE", 6, 2), ("LQ", 1, 0), ("LS", 1, 0), ("LW", 1, 0), ("KB", 1, 1), ("QQ", 0, 0), ("MQ", 2, (4, 8)), ("ET", 3, 0), ("EC", 3, 0), ("ET", 3, 1), ("EC", 3, 1), ("ET", 3, 2), ("EC", 3, 2), ("PC", 4, 2), ("KT", 1, 2), ("KC", 1, 2), ("QP", 1, 0), ("MQ", 3, (0, 4)), ("S1", 2, 0), ("KB", 2, 0), ("S2", 0, 0), ("S1", 2, 1), ("SG", 0, 0), ("S2", 0, 1), ("SG", 0, 1), ("LE", 7, 2), ("KB", 2, 1), ("MQ", 3, (4, 8)), ("YM", 0, 0), ("YM", 0, 1), ("ET", 4, 2), ("QT", 1, 0), ("QC", 1, 0), ("ET", 4, 0), ("ET", 4, 1), ("EC", 4, 1), ("EC", 4, 2), ("EC", 4, 0), ("PC", 5, 2), ("KT", 2, 2), ("KC", 2, 2), ("S1", 3, 0), ("KB", 3, 0), ("MQ", 4, (0, 4)), ("S2", 1, 0), ("S1", 3, 1), ("SG", 1, 0), ("S2", 1, 1), ("SG", 1, 1), ("LE", 8, 2)]
-CLOSING = [("KB", 13, 1), ("MQ", 14, (4, 8)), ("ET", 15, 0), ("EC", 15, 0), ("YM", 11, 0), ("ET", 15, 1), ("EC", 15, 1), ("YM", 11, 1), ("ET", 15, 2), ("EC", 15, 2), ("YT", 4, 2), ("YC", 4, 2), ("SY", 4, 2), ("YT", 4, 3), ("YC", 4, 3), ("SY", 4, 3), ("S1", 14, 0), ("YI", 5, 0), ("MQ", 15, (0, 4)), ("KB", 14, 0), ("S1", 14, 1), ("S2", 12, 0), ("SG", 12, 0), ("S2", 12, 1), ("KT", 13, 2), ("KC", 13, 2), ("SG", 12, 1), ("KB", 14, 1), ("YT", 5, 0), ("YC", 5, 0), ("SY", 5, 0), ("YI", 5, 1), ("MQ", 15, (4, 8)), ("YT", 5, 1), ("YC", 5, 1), ("SY", 5, 1), ("KT", 14, 2), ("KC", 14, 2), ("YT", 5, 2), ("YC", 5, 2), ("SY", 5, 2), ("YT", 5, 3), ("YC", 5, 3), ("SY", 5, 3), ("YQ", 5, 2), ("SW", 5, 0), ("SS", 0, 0), ("MQ", 16, (6, 8)), ("S1", 15, 0), ("KB", 15, 0), ("S1", 15, 1), ("S2", 13, 0), ("SG", 13, 0), ("S2", 13, 1), ("SG", 13, 1), ("S2", 14, 0), ("KT", 15, 0), ("KB", 15, 1), ("YM", 12, 0), ("YM", 12, 1), ("KC", 15, 0), ("KT", 15, 1), ("S2", 14, 1), ("YM", 13, 0), ("MQ", 17, (6, 7)), ("KC", 15, 1), ("SG", 14, 0), ("SG", 14, 1), ("YM", 13, 1), ("MQ", 17, (7, 8)), ("S2", 15, 0), ("SG", 15, 0), ("S2", 15, 1), ("SG", 15, 1), ("YI", 6, 0), ("YM", 14, 0), ("YM", 14, 1), ("YI", 6, 1), ("YT", 6, 0), ("YC", 6, 0), ("SY", 6, 0), ("YT", 6, 1), ("YC", 6, 1), ("SY", 6, 1), ("YT", 6, 2), ("YT", 6, 3), ("YM", 15, 0), ("YM", 15, 1), ("YC", 6, 2), ("SY", 6, 2), ("YQ", 6, 2), ("SW", 6, 0), ("YC", 6, 3), ("SY", 6, 3), ("YT", 7, 0), ("YC", 7, 0), ("SY", 7, 0), ("YT", 7, 1), ("YC", 7, 1), ("SY", 7, 1), ("YI", 7, 0), ("YI", 7, 1), ("YQ", 7, 0), ("YQ", 7, 1), ("SW", 7, 0), ("YT", 7, 2), ("YC", 7, 2), ("SY", 7, 2), ("YT", 7, 3), ("YC", 7, 3), ("SY", 7, 3), ("SS", 1, 0)]
-LIMIT = {"LE": 16, "PC": 16, "ET": 16, "EC": 16, "S1": 16, "KB": 16, "KT": 16, "KC": 16, "S2": 16, "SG": 16, "YM": 16, "MQ": 18,
-         "YI": 8, "YQ": 8, "SW": 8, "YT": 8, "YC": 8, "SY": 8, "LW": 4, "LQ": 4, "QP": 4, "QT": 4, "QC": 4, "QQ": 4}
-
-
-def schedule():
-    steps = list(OPENING)
-    for p in range(FIRST_STEADY, LAST_STEADY + 1):
-        steps += [s for s in steady_round(p) if 0 <= s[1] < LIMIT[s[0]]]
-    return steps + list(CLOSING)
+def split_slots(pair):
+    if pair == 0:
+        return (0, 0)
+    return BOTH if pair % 2 else (0, 1)
 
 
 def tile_cross_layer_key_scores_k7_kernel(
@@ -85,248 +50,385 @@ def tile_cross_layer_key_scores_k7_kernel(
         sb = ctx.enter_context(tc.tile_pool(name="sb", bufs=1))
         ps = ctx.enter_context(tc.psum_pool(name="ps", bufs=1))
 
-        def ring(label, count, shape, dtype):
-            return [sb.tile(shape, dtype, name="%s%d" % (label, i), align_bytes=64) for i in range(count)]
+        def tile(label, shape, dtype):
+            return sb.tile(shape, dtype, name=label, align_bytes=64)
 
-        banks = [ps.tile([P, BANK], F32, name="bank%d" % i) for i in range(BANKS)]
-        ident = sb.tile([P, P], F32, name="ident", align_bytes=64)
-        w_codes = sb.tile([P, G * PASSES, 2 * DK], U8, name="w_codes", align_bytes=64)
-        w_scales = sb.tile([P, G * PASSES, DK], U8, name="w_scales", align_bytes=64)
-        small_rows = sb.tile([P, K_PASS], BF16, name="small_rows", align_bytes=64)
-        small_cols = sb.tile([P, SMALL, PACK], BF16, name="small_cols", align_bytes=64)
-        bias_rows = sb.tile([P, G, DK], BF16, name="bias_rows", align_bytes=64)
-        warm = sb.tile([P, 1], F32, name="warm", align_bytes=64)
-        y_scales = sb.tile([P, HALVES, G * T], U8, name="y_scales", align_bytes=64)
-        q_codes = sb.tile([P, G, T], U32, name="q_codes", align_bytes=64)
-        q_scales = sb.tile([P, G, T], U8, name="q_scales", align_bytes=64)
-        q_split = sb.tile([P, 2, PACK * P], F32, name="q_split", align_bytes=64)
-        q_t = sb.tile([P, 2 * TURNED], BF16, name="q_t", align_bytes=64)
-        y_bf = sb.tile([P, T, PACK], BF16, name="y_bf", align_bytes=64)
-        e_raw = ring("e_raw", R_ERAW, [P, 2, DE], BF16)
-        e_split = ring("e_split", R_ESPLIT, [P, 2, 2 * PASSES * P], F32)
-        stage = ring("stage", R_STAGE, [P, 4 * TURNED], BF16)
-        codes = ring("codes", R_STAGE, [P, TURNED], U32)
-        scales = ring("scales", R_STAGE, [P, TURNED], U8)
+        def ring(label, count, shape, dtype):
+            return [tile("%s%d" % (label, i), shape, dtype) for i in range(count)]
+
+        banks = [ps.tile([P, K_PASS], F32, name="bank%d" % i) for i in range(BANKS)]
+        ident = tile("ident", [P, P], F32)
+        warm = tile("warm", [P, 1], F32)
+        w_codes = tile("w_codes", [P, G * PASSES, 2 * DK], U8)
+        w_scales = tile("w_scales", [P, G * PASSES, DK], U8)
+        small_rows = tile("small_rows", [P, K_PASS], BF16)
+        small_cols = tile("small_cols", [P, SMALL_ROWS, PACK], BF16)
+        bias_rows = tile("bias_rows", [P, G, DK], BF16)
+        y_scales = tile("y_scales", [P, HALVES, G * T], U8)
+        q_codes = tile("q_codes", [P, G, T], U32)
+        q_scales = tile("q_scales", [P, G, T], U8)
+        q_split = tile("q_split", [P, 2, PACK * P], F32)
+        q_turned = tile("q_turned", [P, T * PACK], BF16)
+        y_bf = tile("y_bf", [P, T, PACK], BF16)
+        e_raw = ring("e_raw", RAW_RING, [P, 2, DE], BF16)
+        e_split = ring("e_split", SPLIT_RING, [P, 2, E_BLOCKS * P], F32)
+        stage = ring("stage", STAGE_RING, [P, BLOCKS * K_PASS], BF16)
+        codes = ring("codes", STAGE_RING, [P, BLOCKS * P], U32)
+        scales = ring("scales", STAGE_RING, [P, BLOCKS * P], U8)
         q_raw = ring("q_raw", 2, [P, PACK, DK], BF16)
-        k_rows = ring("k_rows", R_KROWS, [P, 2, DK], BF16)
-        y_st = ring("y_st", R_Y, [P, PACK, T], F32)
+        k_rows = ring("k_rows", KEYS_RING, [P, 2, DK], BF16)
+        y_slots = ring("y_slots", Y_RING, [P, PACK, T], F32)
         y_codes = ring("y_codes", 2, [P, T], U32)
-        y_out = ring("y_out", R_YOUT, [P, K_PASS], F32)
+        y_out = ring("y_out", OUT_RING, [P, 2, K_PASS], F32)
+
+        taken = []
+        sums = {}
+
+        def next_bank():
+            taken.append(banks[len(taken) % BANKS])
+            return taken[-1]
+
+        def turn(sources):
+            bank = next_bank()
+            for i, source in enumerate(sources):
+                nc.tensor.transpose(bank[:, i * P : (i + 1) * P], source, ident[:])
+            return bank
+
+        def join_words(copy, blocks, bank):
+            out = blocks.bitcast(F32).rearrange("q (b r u) -> q b r u", r=P, u=2)
+            copy(out=out, in_=bank[:, : out.shape[1] * 2 * P].rearrange("q (b u r) -> q b r u", r=P, u=2))
+
+        def quantize(words, scale_bytes, values):
+            nc.vector.quantize_mx(out=words.bitcast(FP8X4), scales=scale_bytes, in_=values)
+
+        def load_small():
+            nc.sync.dma_start(out=small_rows[:ROW_KEY_BIAS, :], in_=remap_bias)
+            for row, vec in ((ROW_KEY_BIAS, key_bias), (ROW_KEY_WEIGHT, key_weight)):
+                nc.sync.dma_start(out=small_rows[row : row + UNITS, :], in_=vec.rearrange("h (g s) -> (h g) s", g=HALVES))
+
+        def load_keys(pair, slots=BOTH):
+            unit, first = pair // 2, 2 * (pair % 2)
+            h, g = divmod(unit, HALVES)
+            rows = earlier_keys[h, g * K_PASS : (g + 1) * K_PASS, :].rearrange("(q t) k -> q t k", t=PACK)
+            nc.sync.dma_start(
+                out=e_raw[pair % RAW_RING][:, slots[0] : slots[1], :], in_=rows[:, first + slots[0] : first + slots[1], :]
+            )
+
+        def load_queries(h):
+            nc.sync.dma_start(out=q_raw[h % 2][:], in_=queries[h].rearrange("(b r) k -> r b k", r=P))
+
+        def load_w_codes(h):
+            passes = slice(PASSES * h, PASSES * (h + 1))
+            nc.sync.dma_start(
+                out=w_codes[:, passes, :].bitcast(I32), in_=remap_words.bitcast(I32)[passes, :, :].rearrange("c q n -> q c n")
+            )
+
+        def load_w_scales(passes):
+            for quad in range(4):
+                nc.sync.dma_start(
+                    out=w_scales[32 * quad : 32 * quad + 4, passes, :].bitcast(I32),
+                    in_=remap_scales.bitcast(I32)[passes, 4 * quad : 4 * quad + 4, :].rearrange("c r n -> r c n"),
+                )
+
+        def turn_small():
+            words = small_rows[:].bitcast(F32)
+            bank = turn([words[:, u : 2 * P : 2] for u in range(2)])
+            nc.scalar.copy(
+                out=small_cols[:].bitcast(F32), in_=bank[:, : 2 * P].rearrange("q (u r) -> q r u", u=2)[:, :SMALL_ROWS, :]
+            )
+
+        def spread_bias(h0):
+            words = small_cols[:].bitcast(F32)
+            bank = turn([words[:, h, u : u + 1].to_broadcast([P, P]) for h in (h0, h0 + 1) for u in range(2)])
+            nc.scalar.copy(out=bias_rows[:, h0 : h0 + 2, :].rearrange("p h k -> p (h k)").bitcast(F32), in_=bank[:])
+
+        def split_queries(h):
+            words = q_raw[h % 2][:].rearrange("r b k -> r (b k)").bitcast(F32)
+            nc.vector.tensor_copy(out=q_split[:], in_=words.rearrange("r (m u) -> r u m", u=2))
+
+        def turn_queries(half):
+            bank = turn([q_split[:, u, b * P : (b + 1) * P] for b in (2 * half, 2 * half + 1) for u in range(2)])
+            join_words(nc.scalar.copy, q_turned[:, 2 * half * K_PASS : 2 * (half + 1) * K_PASS], bank)
+
+        def quantize_queries(h):
+            quantize(q_codes[:, h, :], q_scales[:, h, :], q_turned[:])
+
+        def split_keys(pair):
+            lo, hi = split_slots(pair)
+            words = e_raw[pair % RAW_RING][:, lo:hi, :].rearrange("r t k -> r (t k)").bitcast(F32)
+            nc.vector.tensor_copy(
+                out=e_split[pair % SPLIT_RING][:, :, lo * PASSES * P : hi * PASSES * P],
+                in_=words.rearrange("r (m u) -> r u m", u=2),
+            )
+
+        def turn_earlier(pair, third, copy=nc.scalar.copy):
+            sources = []
+            for block in (2 * third, 2 * third + 1):
+                slot, c = divmod(block, PASSES)
+                for u in range(2):
+                    if slot < split_slots(pair)[1]:
+                        sources.append(e_split[pair % SPLIT_RING][:, u, block * P : (block + 1) * P])
+                    else:
+                        words = e_raw[pair % RAW_RING][:, slot, :].bitcast(F32)
+                        sources.append(words[:, 2 * P * c + u : 2 * P * (c + 1) : 2])
+            join_words(copy, stage[pair % STAGE_RING][:, 2 * third * K_PASS : 2 * (third + 1) * K_PASS], turn(sources))
+
+        def quantize_stage(index, lo, hi):
+            cols = slice(lo * P, hi * P)
+            i = index % STAGE_RING
+            quantize(codes[i][:, cols], scales[i][:, cols], stage[i][:, lo * K_PASS : hi * K_PASS])
+
+        def remap(pair, slot):
+            bank = next_bank()
+            for c in range(PASSES):
+                cols = slice((PASSES * slot + c) * P, (PASSES * slot + c + 1) * P)
+                w_pass = PASSES * (pair // PAIRS_PER_HEAD) + c
+                nc.tensor.matmul_mx(
+                    out=bank[:],
+                    lhsT=codes[pair % STAGE_RING][:, cols].bitcast(FP8X4),
+                    lhsT_scale=scales[pair % STAGE_RING][:, cols],
+                    rhs=w_codes[:, w_pass, :].bitcast(FP4X4),
+                    rhs_scale=w_scales[:, w_pass, :],
+                    start=(c == 0),
+                    stop=(c == PASSES - 1),
+                )
+            sums[(pair, slot)] = bank
+
+        def add_bias(pair, slot):
+            nc.vector.tensor_tensor(
+                out=k_rows[pair % KEYS_RING][:, slot, :].rearrange("r (u m e) -> r u m e", u=2, e=2),
+                in0=sums[(pair, slot)][:].rearrange("r (m u e) -> r u m e", u=2, e=2),
+                in1=bias_rows[:, pair // PAIRS_PER_HEAD, :].rearrange("r (u m e) -> r u m e", u=2, e=2),
+                op=mybir.AluOpType.add,
+            )
+
+        def turn_keys(pair, slots=BOTH, copy=nc.scalar.copy):
+            words = k_rows[pair % KEYS_RING][:].bitcast(F32)
+            bank = turn([words[:, slot, u * P : (u + 1) * P] for slot in range(*slots) for u in range(2)])
+            blocks = slice((E_BLOCKS + slots[0]) * K_PASS, (E_BLOCKS + slots[1]) * K_PASS)
+            join_words(copy, stage[(pair + K_LAG) % STAGE_RING][:, blocks], bank)
+
+        def score(pair, slot):
+            unit, t = pair // 2, 2 * (pair % 2) + slot
+            i = (pair + K_LAG) % STAGE_RING
+            cols = slice((E_BLOCKS + slot) * P, (E_BLOCKS + slot + 1) * P)
+            bank = next_bank()
+            nc.tensor.matmul_mx(
+                out=bank[:],
+                lhsT=codes[i][:, cols].bitcast(FP8X4),
+                lhsT_scale=scales[i][:, cols],
+                rhs=q_codes[:, pair // PAIRS_PER_HEAD, :].bitcast(FP8X4),
+                rhs_scale=q_scales[:, pair // PAIRS_PER_HEAD, :],
+                start=True,
+                stop=True,
+            )
+            nc.scalar.activation(
+                out=y_slots[unit % Y_RING][:, t, :],
+                in_=bank[:],
+                func=mybir.ActivationFunctionType.Sigmoid,
+                bias=small_cols[:, ROW_KEY_BIAS + unit, t : t + 1],
+            )
+
+        def weigh(pair, slot):
+            unit, t = pair // 2, 2 * (pair % 2) + slot
+            nc.vector.tensor_scalar(
+                out=y_slots[unit % Y_RING][:, t, :],
+                in0=y_slots[unit % Y_RING][:, t, :],
+                scalar1=small_cols[:, ROW_KEY_WEIGHT + unit, t : t + 1],
+                scalar2=None,
+                op0=mybir.AluOpType.mult,
+            )
+
+        def round_y(unit, half):
+            cols = slice(half * T // 2, (half + 1) * T // 2)
+            nc.vector.tensor_copy(
+                out=y_bf[:, cols, :].rearrange("q (c i) t -> q c t i", i=PACK),
+                in_=y_slots[unit % Y_RING][:, :, cols].rearrange("q t (c i) -> q c t i", i=PACK),
+            )
+
+        def quantize_y(unit, halves=BOTH):
+            h, g = divmod(unit, HALVES)
+            lo, hi = halves[0] * T // 2, halves[1] * T // 2
+            quantize(
+                y_codes[unit % 2][:, lo:hi],
+                y_scales[:, g, h * T + lo : h * T + hi],
+                y_bf[:, lo:hi, :].rearrange("q c t -> q (c t)"),
+            )
+
+        def turn_y(unit, b, copy=nc.scalar.copy):
+            bank = turn([y_slots[unit % Y_RING][:, t, b * P : (b + 1) * P] for t in range(PACK)])
+            copy(
+                out=y_out[(2 * unit + b // 2) % OUT_RING][:, b % 2, :].rearrange("r (q t) -> r q t", t=PACK),
+                in_=bank[:].rearrange("r (t q) -> r q t", t=PACK),
+            )
+
+        def store_y(unit, b, count=2):
+            h, g = divmod(unit, HALVES)
+            rows = out_0[h, b * P : (b + count) * P, g * K_PASS : (g + 1) * K_PASS]
+            nc.sync.dma_start(
+                out=rows.rearrange("(b r) s -> r b s", r=P),
+                in_=y_out[(2 * unit + b // 2) % OUT_RING][:, b % 2 : b % 2 + count, :],
+            )
+
+        def store_codes(unit):
+            h, g = divmod(unit, HALVES)
+            words = out_1[g].rearrange("q m t -> q (m t)").bitcast(I32)
+            nc.sync.dma_start(out=words[:, h * T : (h + 1) * T], in_=y_codes[unit % 2][:].bitcast(I32))
+
+        def store_scales(h_lo, h_hi, queues):
+            cols = slice(h_lo * T // 4, h_hi * T // 4)
+            for quad in range(4):
+                queues[quad % len(queues)].dma_start(
+                    out=out_2.bitcast(I32)[:, 4 * quad : 4 * quad + 4, cols].rearrange("g r m -> r g m"),
+                    in_=y_scales[32 * quad : 32 * quad + 4, :, :].bitcast(I32)[:, :, cols],
+                )
+
+        def pipeline_round(p):
+            unit, second = divmod(p - 6, 2)
+            h, phase = divmod(p, PAIRS_PER_HEAD)
+            turn_earlier(p + 1, 0)
+            if p >= 1:
+                add_bias(p - 1, 1)
+            if phase == 2:
+                quantize_queries(h)
+            turn_earlier(p + 1, 1)
+            turn_earlier(p + 1, 2, nc.scalar.copy if p + 2 < PAIRS else nc.vector.tensor_copy)
+            if p >= 2:
+                turn_keys(p - 2)
+            if unit >= 0 and second:
+                quantize_y(unit)
+                store_codes(unit)
+            if phase == 1:
+                turn_queries(0)
+                turn_queries(1)
+            if unit >= 0:
+                turn_y(unit, 2 * second)
+                turn_y(unit, 2 * second + 1)
+            if p + 2 < PAIRS:
+                split_keys(p + 2)
+            if p >= 4:
+                weigh(p - 4, 0)
+                weigh(p - 4, 1)
+            if phase == 0:
+                split_queries(h)
+            if p >= 3:
+                score(p - 3, 0)
+                score(p - 3, 1)
+            if unit >= 0 and not second:
+                round_y(unit, 1)
+            if p + 1 < K_LAG:
+                for third in range(PASSES):
+                    quantize_stage(p + 1, 2 * third, 2 * third + 2)
+            else:
+                quantize_stage(p + 1, 0, BLOCKS)
+            if unit >= 0 and not second:
+                round_y(unit, 0)
+            if p >= 0:
+                remap(p, 0)
+                remap(p, 1)
+                add_bias(p, 0)
+            if unit >= 0:
+                store_y(unit, 2 * second)
+            if p + RAW_RING < PAIRS:
+                load_keys(p + RAW_RING)
+            if phase == 1 and h + 1 < G:
+                load_queries(h + 1)
+                load_w_codes(h + 1)
 
         ctx.enter_context(tc.manual_schedule())
 
         nc.vector.memset(warm[:], 0.0)
+        nc.scalar.activation(out=warm[:], in_=warm[:], func=mybir.ActivationFunctionType.Sigmoid)
+
         nc.vector.memset(small_rows[:].bitcast(I32), 0)
-        nc.vector.memset(w_scales[:, :PASSES, :].rearrange("p g n -> p (g n)").bitcast(I32), 0)
-        nc.vector.memset(w_scales[:, PASSES:, :].rearrange("p g n -> p (g n)").bitcast(I32), 0)
+        nc.vector.memset(w_scales[:, :PASSES, :].rearrange("q c n -> q (c n)").bitcast(I32), 0)
+        nc.vector.memset(w_scales[:, PASSES:, :].rearrange("q c n -> q (c n)").bitcast(I32), 0)
         make_identity(nc, ident[:])
-        nc.scalar.activation(out=warm[:], in_=warm[:], func=ACT.Sigmoid)
 
-        held = {}
-        used = []
+        load_small()
+        load_keys(0, (0, 1))
+        load_keys(0, (1, 2))
+        load_keys(1)
+        load_w_scales(slice(0, PASSES))
+        load_w_codes(0)
+        load_keys(2)
+        turn_small()
+        load_queries(0)
+        load_keys(3)
+        pipeline_round(-1)
+        spread_bias(0)
+        spread_bias(2)
+        load_w_scales(slice(PASSES, G * PASSES))
+        for p in range(PAIRS - 1):
+            pipeline_round(p)
 
-        def take_bank(kind, n, j):
-            bank = banks[len(used) % BANKS]
-            used.append(kind)
-            held[(kind, n, j)] = bank
-            return bank
+        add_bias(14, 1)
+        turn_keys(13)
+        turn_y(4, 2)
+        turn_y(4, 3)
+        weigh(11, 0)
+        weigh(11, 1)
+        quantize_y(4)
+        store_codes(4)
+        store_y(4, 2)
+        score(12, 0)
+        score(12, 1)
+        remap(15, 0)
+        add_bias(15, 0)
+        quantize_stage(13 + K_LAG, E_BLOCKS, BLOCKS)
 
-        def turn_words(bank, blocks):
-            for i, block in enumerate(blocks):
-                nc.tensor.transpose(bank[:, i * P : (i + 1) * P], block, ident[:])
+        turn_keys(14)
+        turn_y(5, 0)
+        turn_y(5, 1)
+        remap(15, 1)
+        score(13, 0)
+        score(13, 1)
+        weigh(12, 0)
+        round_y(5, 0)
+        round_y(5, 1)
+        add_bias(15, 1)
+        weigh(12, 1)
 
-        def join_words(eng, dst, bank):
-            out = dst.bitcast(F32).rearrange("p (j r u) -> p j r u", r=P, u=2)
-            src = bank[:, : out.shape[1] * 2 * P].rearrange("p (j u r) -> p j r u", r=P, u=2)
-            if eng == "act":
-                nc.scalar.copy(out=out, in_=src)
-            else:
-                nc.vector.tensor_copy(out=out, in_=src)
+        turn_keys(15, (0, 1), nc.vector.tensor_copy)
+        store_y(5, 0)
+        quantize_stage(14 + K_LAG, E_BLOCKS, BLOCKS)
+        quantize_y(5)
+        store_codes(5)
+        turn_y(5, 2)
+        turn_keys(15, (1, 2))
+        turn_y(5, 3)
+        weigh(13, 0)
+        weigh(13, 1)
+        score(14, 0)
+        score(14, 1)
+        quantize_stage(15 + K_LAG, E_BLOCKS, E_BLOCKS + 1)
+        quantize_stage(15 + K_LAG, E_BLOCKS + 1, BLOCKS)
+        score(15, 0)
+        score(15, 1)
+        store_y(5, 2)
+        store_scales(0, G - 1, [nc.sync])
 
-        def quantize(words, scale_bytes, src):
-            nc.vector.quantize_mx(out=words.bitcast(FP8X4), scales=scale_bytes, in_=src)
-
-        def copy_on(eng, out, src):
-            if eng == "act":
-                nc.scalar.copy(out=out, in_=src)
-            else:
-                nc.vector.tensor_copy(out=out, in_=src)
-
-        for kind, n, j in schedule():
-            h, g = divmod(n, HALVES)
-            unit, hf = divmod(n, 2)
-            slots = slice(0, 2) if j == 2 else slice(j, j + 1) if kind in ("LE", "PC", "YQ", "KT", "KC") else None
-            if kind == "LE":
-                head, half = divmod(unit, HALVES)
-                rows = earlier_keys[head, half * K_PASS : (half + 1) * K_PASS, :].rearrange("(p t) k -> p t k", t=PACK)
-                nc.sync.dma_start(out=e_raw[n % R_ERAW][:, slots, :], in_=rows[:, 2 * hf + slots.start : 2 * hf + slots.stop, :])
-            elif kind == "LQ":
-                nc.sync.dma_start(out=q_raw[n % 2][:], in_=queries[n].rearrange("(b r) k -> r b k", r=P))
-            elif kind == "LW":
-                nc.sync.dma_start(
-                    out=w_codes[:, PASSES * n : PASSES * (n + 1), :].bitcast(I32),
-                    in_=remap_words.bitcast(I32)[PASSES * n : PASSES * (n + 1), :, :].rearrange("g p n -> p g n"),
-                )
-            elif kind == "LC":
-                nc.gpsimd.dma_start(out=small_rows[0:G, :], in_=remap_bias)
-                nc.gpsimd.dma_start(
-                    out=small_rows[G : G + UNITS, :], in_=key_bias.rearrange("h (g s) -> (h g) s", g=HALVES)
-                )
-                nc.gpsimd.dma_start(
-                    out=small_rows[G + UNITS : SMALL, :], in_=key_weight.rearrange("h (g s) -> (h g) s", g=HALVES)
-                )
-            elif kind == "LS":
-                groups = slice(0, PASSES) if n == 0 else slice(PASSES, G * PASSES)
-                for quad in range(4):
-                    nc.sync.dma_start(
-                        out=w_scales[32 * quad : 32 * quad + 4, groups, :].bitcast(I32),
-                        in_=remap_scales.bitcast(I32)[groups, 4 * quad : 4 * quad + 4, :].rearrange("g r n -> r g n"),
-                    )
-            elif kind == "CT":
-                words = small_rows[:].bitcast(F32)
-                turn_words(take_bank(kind, n, j), [words[:, u : 2 * P : 2] for u in range(2)])
-            elif kind == "CC":
-                nc.scalar.copy(
-                    out=small_cols[:].bitcast(F32),
-                    in_=held[("CT", n, j)][:, : 2 * P].rearrange("p (u r) -> p r u", u=2)[:, :SMALL, :],
-                )
-            elif kind == "PC":
-                cols = slice(slots.start * PASSES * P, slots.stop * PASSES * P)
-                words = e_raw[n % R_ERAW][:, slots, :].rearrange("p t k -> p (t k)").bitcast(F32)
-                copy_on(copy_engine(kind, n, j), e_split[n % R_ESPLIT][:, :, cols], words.rearrange("p (m u) -> p u m", u=2))
-            elif kind == "QP":
-                words = q_raw[n % 2][:].rearrange("p b k -> p (b k)").bitcast(F32)
-                copy_on(copy_engine(kind, n, j), q_split[:], words.rearrange("p (m u) -> p u m", u=2))
-            elif kind == "ET":
-                blocks = []
-                for jj in (2 * j, 2 * j + 1):
-                    t, c = divmod(jj, PASSES)
-                    for u in range(2):
-                        if n > 0:
-                            blocks.append(e_split[n % R_ESPLIT][:, u, jj * P : (jj + 1) * P])
-                        else:
-                            words = e_raw[n % R_ERAW][:, t, :].bitcast(F32)
-                            blocks.append(words[:, 2 * P * c + u : 2 * P * (c + 1) : 2])
-                turn_words(take_bank(kind, n, j), blocks)
-            elif kind == "EC":
-                join_words(copy_engine(kind, n, j), stage[n % R_STAGE][:, j * TURNED : (j + 1) * TURNED], held[("ET", n, j)])
-            elif kind == "MQ":
-                cols = slice(P * j[0], P * j[1])
-                quantize(
-                    codes[n % R_STAGE][:, cols],
-                    scales[n % R_STAGE][:, cols],
-                    stage[n % R_STAGE][:, j[0] * K_PASS : j[1] * K_PASS],
-                )
-            elif kind == "S1":
-                bank = take_bank(kind, n, j)
-                for c in range(PASSES):
-                    cols = slice((PASSES * j + c) * P, (PASSES * j + c + 1) * P)
-                    nc.tensor.matmul_mx(
-                        out=bank[:],
-                        lhsT=codes[n % R_STAGE][:, cols].bitcast(FP8X4),
-                        lhsT_scale=scales[n % R_STAGE][:, cols],
-                        rhs=w_codes[:, PASSES * (n // 4) + c, :].bitcast(FP4X4),
-                        rhs_scale=w_scales[:, PASSES * (n // 4) + c, :],
-                        start=(c == 0),
-                        stop=(c == PASSES - 1),
-                    )
-            elif kind == "KB":
-                nc.vector.tensor_tensor(
-                    out=k_rows[n % R_KROWS][:, j, :].rearrange("p (u m e) -> p u m e", u=2, e=2),
-                    in0=held[("S1", n, j)][:].rearrange("p (m u e) -> p u m e", u=2, e=2),
-                    in1=bias_rows[:, n // 4, :].rearrange("p (u m e) -> p u m e", u=2, e=2),
-                    op=ALU.add,
-                )
-            elif kind == "KT":
-                blocks = []
-                for t in range(slots.start, slots.stop):
-                    words = k_rows[n % R_KROWS][:, t, :].bitcast(F32)
-                    for u in range(2):
-                        blocks.append(words[:, u * P : (u + 1) * P])
-                turn_words(take_bank(kind, n, j), blocks)
-            elif kind == "KC":
-                join_words(copy_engine(kind, n, j), stage[(n + K_LAG) % R_STAGE][:, (6 + slots.start) * K_PASS : (6 + slots.stop) * K_PASS], held[("KT", n, j)])
-            elif kind == "QT":
-                blocks = []
-                for b in (2 * j, 2 * j + 1):
-                    for u in range(2):
-                        blocks.append(q_split[:, u, b * P : (b + 1) * P])
-                turn_words(take_bank(kind, n, j), blocks)
-            elif kind == "QC":
-                join_words(copy_engine(kind, n, j), q_t[:, j * TURNED : (j + 1) * TURNED], held[("QT", n, j)])
-            elif kind == "QQ":
-                quantize(q_codes[:, n, :], q_scales[:, n, :], q_t[:])
-            elif kind == "S2":
-                cols = slice((6 + j) * P, (7 + j) * P)
-                nc.tensor.matmul_mx(
-                    out=take_bank(kind, n, j)[:],
-                    lhsT=codes[(n + K_LAG) % R_STAGE][:, cols].bitcast(FP8X4),
-                    lhsT_scale=scales[(n + K_LAG) % R_STAGE][:, cols],
-                    rhs=q_codes[:, n // 4, :].bitcast(FP8X4),
-                    rhs_scale=q_scales[:, n // 4, :],
-                    start=True,
-                    stop=True,
-                )
-            elif kind == "SG":
-                t = 2 * hf + j
-                nc.scalar.activation(
-                    out=y_st[unit % R_Y][:, t, :],
-                    in_=held[("S2", n, j)][:],
-                    func=ACT.Sigmoid,
-                    bias=small_cols[:, G + unit, t : t + 1],
-                )
-            elif kind == "YM":
-                t = 2 * hf + j
-                nc.vector.tensor_scalar(
-                    out=y_st[unit % R_Y][:, t, :],
-                    in0=y_st[unit % R_Y][:, t, :],
-                    scalar1=small_cols[:, G + UNITS + unit, t : t + 1],
-                    scalar2=None,
-                    op0=ALU.mult,
-                )
-            elif kind == "YI":
-                cols = slice(j * T // 2, (j + 1) * T // 2)
-                nc.vector.tensor_copy(
-                    out=y_bf[:, cols, :].rearrange("p (c i) t -> p c t i", i=PACK),
-                    in_=y_st[n % R_Y][:, :, cols].rearrange("p t (c i) -> p c t i", i=PACK),
-                )
-            elif kind == "YQ":
-                cols = slice(slots.start * T // 2, slots.stop * T // 2)
-                quantize(
-                    y_codes[n % 2][:, cols],
-                    y_scales[:, g, h * T + cols.start : h * T + cols.stop],
-                    y_bf[:, cols, :].rearrange("p c t -> p (c t)"),
-                )
-            elif kind == "SW":
-                words = out_1[g].rearrange("p m t -> p (m t)").bitcast(I32)
-                nc.sync.dma_start(out=words[:, h * T : (h + 1) * T], in_=y_codes[n % 2][:].bitcast(I32))
-            elif kind == "SS":
-                cols = slice(0, (G - 1) * T // 4) if n == 0 else slice((G - 1) * T // 4, G * T // 4)
-                for quad in range(4):
-                    queue = nc.scalar if n == 1 and quad % 2 else nc.sync
-                    queue.dma_start(
-                        out=out_2.bitcast(I32)[:, 4 * quad : 4 * quad + 4, cols].rearrange("g r m -> r g m"),
-                        in_=y_scales[32 * quad : 32 * quad + 4, :, :].bitcast(I32)[:, :, cols],
-                    )
-            elif kind == "YT":
-                turn_words(take_bank(kind, n, j), [y_st[n % R_Y][:, t, j * P : (j + 1) * P] for t in range(PACK)])
-            elif kind == "YC":
-                copy_on(
-                    copy_engine(kind, n, j),
-                    y_out[(PACK * n + j) % R_YOUT][:].rearrange("r (p t) -> r p t", t=PACK),
-                    held[("YT", n, j)][:].rearrange("r (t p) -> r p t", t=PACK),
-                )
-            elif kind == "SY":
-                nc.sync.dma_start(
-                    out=out_0[h, j * P : (j + 1) * P, g * K_PASS : (g + 1) * K_PASS], in_=y_out[(PACK * n + j) % R_YOUT][:]
-                )
-            elif kind == "BT":
-                words = small_cols[:].bitcast(F32)
-                blocks = [words[:, hh, u : u + 1].to_broadcast([P, P]) for hh in (2 * j, 2 * j + 1) for u in range(2)]
-                turn_words(take_bank(kind, n, j), blocks)
-            elif kind == "BC":
-                copy_on(
-                    copy_engine(kind, n, j),
-                    bias_rows[:, 2 * j : 2 * j + 2, :].rearrange("p h k -> p (h k)").bitcast(F32),
-                    held[("BT", n, j)][:],
-                )
+        for half in range(2):
+            round_y(6, half)
+        for half in range(2):
+            quantize_y(6, (half, half + 1))
+        store_codes(6)
+        for b in range(PACK):
+            turn_y(6, b)
+        for pair in (14, 15):
+            weigh(pair, 0)
+            weigh(pair, 1)
+        store_y(6, 0)
+        store_y(6, 2)
+        for half in range(2):
+            round_y(7, half)
+        for half in range(2):
+            quantize_y(7, (half, half + 1))
+        for b in range(PACK - 1):
+            turn_y(7, b)
+        turn_y(7, PACK - 1, nc.vector.tensor_copy)
+        store_y(7, 0)
+        store_codes(7)
+        store_scales(G - 1, G, [nc.sync])
+        store_y(7, 2, 1)
+        store_y(7, 3, 1)

from contextlib import ExitStack

import concourse.mybir as mybir
from concourse.masks import make_identity

G, S, T, DE, DK = 4, 1024, 512, 1536, 512
FLOPS = 2 * G * S * DK * (DE + T)

F32 = mybir.dt.float32
BF16 = mybir.dt.bfloat16
I32 = mybir.dt.int32
U32 = mybir.dt.uint32
U8 = mybir.dt.uint8
FP8X4 = mybir.dt.float8_e4m3fn_x4
FP4X4 = mybir.dt.float4_e2m1fn_x4

P = 128
PACK = 4
K_PASS = P * PACK
PASSES = DE // K_PASS
HALVES = S // K_PASS
UNITS = G * HALVES
PAIRS = 2 * UNITS
PAIRS_PER_HEAD = PAIRS // G
BANKS = 8
BOTH = (0, 2)

E_BLOCKS = 2 * PASSES
BLOCKS = E_BLOCKS + 2
K_LAG = 3

ROW_KEY_BIAS = G
ROW_KEY_WEIGHT = G + UNITS
SMALL_ROWS = G + 2 * UNITS

RAW_RING, SPLIT_RING, STAGE_RING, KEYS_RING, Y_RING, OUT_RING = 5, 3, 3, 3, 4, 4


def split_slots(pair):
    if pair == 0:
        return (0, 0)
    return BOTH if pair % 2 else (0, 1)


def tile_cross_layer_key_scores_k7_kernel(
    tc, earlier_keys, remap_words, remap_scales, remap_bias, queries, key_bias, key_weight, out_0, out_1, out_2
):
    nc = tc.nc
    with ExitStack() as ctx:
        sb = ctx.enter_context(tc.tile_pool(name="sb", bufs=1))
        ps = ctx.enter_context(tc.psum_pool(name="ps", bufs=1))

        def tile(label, shape, dtype):
            return sb.tile(shape, dtype, name=label, align_bytes=64)

        def ring(label, count, shape, dtype):
            return [tile("%s%d" % (label, i), shape, dtype) for i in range(count)]

        banks = [ps.tile([P, K_PASS], F32, name="bank%d" % i) for i in range(BANKS)]
        ident = tile("ident", [P, P], F32)
        warm = tile("warm", [P, 1], F32)
        w_codes = tile("w_codes", [P, G * PASSES, 2 * DK], U8)
        w_scales = tile("w_scales", [P, G * PASSES, DK], U8)
        small_rows = tile("small_rows", [P, K_PASS], BF16)
        small_cols = tile("small_cols", [P, SMALL_ROWS, PACK], BF16)
        bias_rows = tile("bias_rows", [P, G, DK], BF16)
        y_scales = tile("y_scales", [P, HALVES, G * T], U8)
        q_codes = tile("q_codes", [P, G, T], U32)
        q_scales = tile("q_scales", [P, G, T], U8)
        q_split = tile("q_split", [P, 2, PACK * P], F32)
        q_turned = tile("q_turned", [P, T * PACK], BF16)
        y_bf = tile("y_bf", [P, T, PACK], BF16)
        e_raw = ring("e_raw", RAW_RING, [P, 2, DE], BF16)
        e_split = ring("e_split", SPLIT_RING, [P, 2, E_BLOCKS * P], F32)
        stage = ring("stage", STAGE_RING, [P, BLOCKS * K_PASS], BF16)
        codes = ring("codes", STAGE_RING, [P, BLOCKS * P], U32)
        scales = ring("scales", STAGE_RING, [P, BLOCKS * P], U8)
        q_raw = ring("q_raw", 2, [P, PACK, DK], BF16)
        k_rows = ring("k_rows", KEYS_RING, [P, 2, DK], BF16)
        y_slots = ring("y_slots", Y_RING, [P, PACK, T], F32)
        y_codes = ring("y_codes", 2, [P, T], U32)
        y_out = ring("y_out", OUT_RING, [P, 2, K_PASS], F32)

        taken = []
        sums = {}

        def next_bank():
            taken.append(banks[len(taken) % BANKS])
            return taken[-1]

        def turn(sources):
            bank = next_bank()
            for i, source in enumerate(sources):
                nc.tensor.transpose(bank[:, i * P : (i + 1) * P], source, ident[:])
            return bank

        def join_words(copy, blocks, bank):
            out = blocks.bitcast(F32).rearrange("q (b r u) -> q b r u", r=P, u=2)
            copy(out=out, in_=bank[:, : out.shape[1] * 2 * P].rearrange("q (b u r) -> q b r u", r=P, u=2))

        def quantize(words, scale_bytes, values):
            nc.vector.quantize_mx(out=words.bitcast(FP8X4), scales=scale_bytes, in_=values)

        def load_small():
            nc.sync.dma_start(out=small_rows[:ROW_KEY_BIAS, :], in_=remap_bias)
            for row, vec in ((ROW_KEY_BIAS, key_bias), (ROW_KEY_WEIGHT, key_weight)):
                nc.sync.dma_start(out=small_rows[row : row + UNITS, :], in_=vec.rearrange("h (g s) -> (h g) s", g=HALVES))

        def load_keys(pair, slots=BOTH):
            unit, first = pair // 2, 2 * (pair % 2)
            h, g = divmod(unit, HALVES)
            rows = earlier_keys[h, g * K_PASS : (g + 1) * K_PASS, :].rearrange("(q t) k -> q t k", t=PACK)
            nc.sync.dma_start(
                out=e_raw[pair % RAW_RING][:, slots[0] : slots[1], :], in_=rows[:, first + slots[0] : first + slots[1], :]
            )

        def load_queries(h):
            nc.sync.dma_start(out=q_raw[h % 2][:], in_=queries[h].rearrange("(b r) k -> r b k", r=P))

        def load_w_codes(h):
            passes = slice(PASSES * h, PASSES * (h + 1))
            nc.sync.dma_start(
                out=w_codes[:, passes, :].bitcast(I32), in_=remap_words.bitcast(I32)[passes, :, :].rearrange("c q n -> q c n")
            )

        def load_w_scales(passes):
            for quad in range(4):
                nc.sync.dma_start(
                    out=w_scales[32 * quad : 32 * quad + 4, passes, :].bitcast(I32),
                    in_=remap_scales.bitcast(I32)[passes, 4 * quad : 4 * quad + 4, :].rearrange("c r n -> r c n"),
                )

        def turn_small():
            words = small_rows[:].bitcast(F32)
            bank = turn([words[:, u : 2 * P : 2] for u in range(2)])
            nc.scalar.copy(
                out=small_cols[:].bitcast(F32), in_=bank[:, : 2 * P].rearrange("q (u r) -> q r u", u=2)[:, :SMALL_ROWS, :]
            )

        def spread_bias(h0):
            words = small_cols[:].bitcast(F32)
            bank = turn([words[:, h, u : u + 1].to_broadcast([P, P]) for h in (h0, h0 + 1) for u in range(2)])
            nc.scalar.copy(out=bias_rows[:, h0 : h0 + 2, :].rearrange("p h k -> p (h k)").bitcast(F32), in_=bank[:])

        def split_queries(h):
            words = q_raw[h % 2][:].rearrange("r b k -> r (b k)").bitcast(F32)
            nc.vector.tensor_copy(out=q_split[:], in_=words.rearrange("r (m u) -> r u m", u=2))

        def turn_queries(half):
            bank = turn([q_split[:, u, b * P : (b + 1) * P] for b in (2 * half, 2 * half + 1) for u in range(2)])
            join_words(nc.scalar.copy, q_turned[:, 2 * half * K_PASS : 2 * (half + 1) * K_PASS], bank)

        def quantize_queries(h):
            quantize(q_codes[:, h, :], q_scales[:, h, :], q_turned[:])

        def split_keys(pair):
            lo, hi = split_slots(pair)
            words = e_raw[pair % RAW_RING][:, lo:hi, :].rearrange("r t k -> r (t k)").bitcast(F32)
            nc.vector.tensor_copy(
                out=e_split[pair % SPLIT_RING][:, :, lo * PASSES * P : hi * PASSES * P],
                in_=words.rearrange("r (m u) -> r u m", u=2),
            )

        def turn_earlier(pair, third, copy=nc.scalar.copy):
            sources = []
            for block in (2 * third, 2 * third + 1):
                slot, c = divmod(block, PASSES)
                for u in range(2):
                    if slot < split_slots(pair)[1]:
                        sources.append(e_split[pair % SPLIT_RING][:, u, block * P : (block + 1) * P])
                    else:
                        words = e_raw[pair % RAW_RING][:, slot, :].bitcast(F32)
                        sources.append(words[:, 2 * P * c + u : 2 * P * (c + 1) : 2])
            join_words(copy, stage[pair % STAGE_RING][:, 2 * third * K_PASS : 2 * (third + 1) * K_PASS], turn(sources))

        def quantize_stage(index, lo, hi):
            cols = slice(lo * P, hi * P)
            i = index % STAGE_RING
            quantize(codes[i][:, cols], scales[i][:, cols], stage[i][:, lo * K_PASS : hi * K_PASS])

        def remap(pair, slot):
            bank = next_bank()
            for c in range(PASSES):
                cols = slice((PASSES * slot + c) * P, (PASSES * slot + c + 1) * P)
                w_pass = PASSES * (pair // PAIRS_PER_HEAD) + c
                nc.tensor.matmul_mx(
                    out=bank[:],
                    lhsT=codes[pair % STAGE_RING][:, cols].bitcast(FP8X4),
                    lhsT_scale=scales[pair % STAGE_RING][:, cols],
                    rhs=w_codes[:, w_pass, :].bitcast(FP4X4),
                    rhs_scale=w_scales[:, w_pass, :],
                    start=(c == 0),
                    stop=(c == PASSES - 1),
                )
            sums[(pair, slot)] = bank

        def add_bias(pair, slot):
            nc.vector.tensor_tensor(
                out=k_rows[pair % KEYS_RING][:, slot, :].rearrange("r (u m e) -> r u m e", u=2, e=2),
                in0=sums[(pair, slot)][:].rearrange("r (m u e) -> r u m e", u=2, e=2),
                in1=bias_rows[:, pair // PAIRS_PER_HEAD, :].rearrange("r (u m e) -> r u m e", u=2, e=2),
                op=mybir.AluOpType.add,
            )

        def turn_keys(pair, slots=BOTH, copy=nc.scalar.copy):
            words = k_rows[pair % KEYS_RING][:].bitcast(F32)
            bank = turn([words[:, slot, u * P : (u + 1) * P] for slot in range(*slots) for u in range(2)])
            blocks = slice((E_BLOCKS + slots[0]) * K_PASS, (E_BLOCKS + slots[1]) * K_PASS)
            join_words(copy, stage[(pair + K_LAG) % STAGE_RING][:, blocks], bank)

        def score(pair, slot):
            unit, t = pair // 2, 2 * (pair % 2) + slot
            i = (pair + K_LAG) % STAGE_RING
            cols = slice((E_BLOCKS + slot) * P, (E_BLOCKS + slot + 1) * P)
            bank = next_bank()
            nc.tensor.matmul_mx(
                out=bank[:],
                lhsT=codes[i][:, cols].bitcast(FP8X4),
                lhsT_scale=scales[i][:, cols],
                rhs=q_codes[:, pair // PAIRS_PER_HEAD, :].bitcast(FP8X4),
                rhs_scale=q_scales[:, pair // PAIRS_PER_HEAD, :],
                start=True,
                stop=True,
            )
            nc.scalar.activation(
                out=y_slots[unit % Y_RING][:, t, :],
                in_=bank[:],
                func=mybir.ActivationFunctionType.Sigmoid,
                bias=small_cols[:, ROW_KEY_BIAS + unit, t : t + 1],
            )

        def weigh(pair, slot):
            unit, t = pair // 2, 2 * (pair % 2) + slot
            nc.vector.tensor_scalar(
                out=y_slots[unit % Y_RING][:, t, :],
                in0=y_slots[unit % Y_RING][:, t, :],
                scalar1=small_cols[:, ROW_KEY_WEIGHT + unit, t : t + 1],
                scalar2=None,
                op0=mybir.AluOpType.mult,
            )

        def round_y(unit, half):
            cols = slice(half * T // 2, (half + 1) * T // 2)
            nc.vector.tensor_copy(
                out=y_bf[:, cols, :].rearrange("q (c i) t -> q c t i", i=PACK),
                in_=y_slots[unit % Y_RING][:, :, cols].rearrange("q t (c i) -> q c t i", i=PACK),
            )

        def quantize_y(unit, halves=BOTH):
            h, g = divmod(unit, HALVES)
            lo, hi = halves[0] * T // 2, halves[1] * T // 2
            quantize(
                y_codes[unit % 2][:, lo:hi],
                y_scales[:, g, h * T + lo : h * T + hi],
                y_bf[:, lo:hi, :].rearrange("q c t -> q (c t)"),
            )

        def turn_y(unit, b, copy=nc.scalar.copy):
            bank = turn([y_slots[unit % Y_RING][:, t, b * P : (b + 1) * P] for t in range(PACK)])
            copy(
                out=y_out[(2 * unit + b // 2) % OUT_RING][:, b % 2, :].rearrange("r (q t) -> r q t", t=PACK),
                in_=bank[:].rearrange("r (t q) -> r q t", t=PACK),
            )

        def store_y(unit, b, count=2):
            h, g = divmod(unit, HALVES)
            rows = out_0[h, b * P : (b + count) * P, g * K_PASS : (g + 1) * K_PASS]
            nc.sync.dma_start(
                out=rows.rearrange("(b r) s -> r b s", r=P),
                in_=y_out[(2 * unit + b // 2) % OUT_RING][:, b % 2 : b % 2 + count, :],
            )

        def store_codes(unit):
            h, g = divmod(unit, HALVES)
            words = out_1[g].rearrange("q m t -> q (m t)").bitcast(I32)
            nc.sync.dma_start(out=words[:, h * T : (h + 1) * T], in_=y_codes[unit % 2][:].bitcast(I32))

        def store_scales(h_lo, h_hi, queues):
            cols = slice(h_lo * T // 4, h_hi * T // 4)
            for quad in range(4):
                queues[quad % len(queues)].dma_start(
                    out=out_2.bitcast(I32)[:, 4 * quad : 4 * quad + 4, cols].rearrange("g r m -> r g m"),
                    in_=y_scales[32 * quad : 32 * quad + 4, :, :].bitcast(I32)[:, :, cols],
                )

        def pipeline_round(p):
            unit, second = divmod(p - 6, 2)
            h, phase = divmod(p, PAIRS_PER_HEAD)
            turn_earlier(p + 1, 0)
            if p >= 1:
                add_bias(p - 1, 1)
            if phase == 2:
                quantize_queries(h)
            turn_earlier(p + 1, 1)
            turn_earlier(p + 1, 2, nc.scalar.copy if p + 2 < PAIRS else nc.vector.tensor_copy)
            if p >= 2:
                turn_keys(p - 2)
            if unit >= 0 and second:
                quantize_y(unit)
                store_codes(unit)
            if phase == 1:
                turn_queries(0)
                turn_queries(1)
            if unit >= 0:
                turn_y(unit, 2 * second)
                turn_y(unit, 2 * second + 1)
            if p + 2 < PAIRS:
                split_keys(p + 2)
            if p >= 4:
                weigh(p - 4, 0)
                weigh(p - 4, 1)
            if phase == 0:
                split_queries(h)
            if p >= 3:
                score(p - 3, 0)
                score(p - 3, 1)
            if unit >= 0 and not second:
                round_y(unit, 1)
            if p + 1 < K_LAG:
                for third in range(PASSES):
                    quantize_stage(p + 1, 2 * third, 2 * third + 2)
            else:
                quantize_stage(p + 1, 0, BLOCKS)
            if unit >= 0 and not second:
                round_y(unit, 0)
            if p >= 0:
                remap(p, 0)
                remap(p, 1)
                add_bias(p, 0)
            if unit >= 0:
                store_y(unit, 2 * second)
            if p + RAW_RING < PAIRS:
                load_keys(p + RAW_RING)
            if phase == 1 and h + 1 < G:
                load_queries(h + 1)
                load_w_codes(h + 1)

        ctx.enter_context(tc.manual_schedule())

        nc.vector.memset(warm[:], 0.0)
        nc.scalar.activation(out=warm[:], in_=warm[:], func=mybir.ActivationFunctionType.Sigmoid)

        nc.vector.memset(small_rows[:].bitcast(I32), 0)
        nc.vector.memset(w_scales[:, :PASSES, :].rearrange("q c n -> q (c n)").bitcast(I32), 0)
        nc.vector.memset(w_scales[:, PASSES:, :].rearrange("q c n -> q (c n)").bitcast(I32), 0)
        make_identity(nc, ident[:])

        load_small()
        load_keys(0, (0, 1))
        load_keys(0, (1, 2))
        load_keys(1)
        load_w_scales(slice(0, PASSES))
        load_w_codes(0)
        load_keys(2)
        turn_small()
        load_queries(0)
        load_keys(3)
        pipeline_round(-1)
        spread_bias(0)
        spread_bias(2)
        load_w_scales(slice(PASSES, G * PASSES))
        for p in range(PAIRS - 1):
            pipeline_round(p)

        add_bias(14, 1)
        turn_keys(13)
        turn_y(4, 2)
        turn_y(4, 3)
        weigh(11, 0)
        weigh(11, 1)
        quantize_y(4)
        store_codes(4)
        store_y(4, 2)
        score(12, 0)
        score(12, 1)
        remap(15, 0)
        add_bias(15, 0)
        quantize_stage(13 + K_LAG, E_BLOCKS, BLOCKS)

        turn_keys(14)
        turn_y(5, 0)
        turn_y(5, 1)
        remap(15, 1)
        score(13, 0)
        score(13, 1)
        weigh(12, 0)
        round_y(5, 0)
        round_y(5, 1)
        add_bias(15, 1)
        weigh(12, 1)

        turn_keys(15, (0, 1), nc.vector.tensor_copy)
        store_y(5, 0)
        quantize_stage(14 + K_LAG, E_BLOCKS, BLOCKS)
        quantize_y(5)
        store_codes(5)
        turn_y(5, 2)
        turn_keys(15, (1, 2))
        turn_y(5, 3)
        weigh(13, 0)
        weigh(13, 1)
        score(14, 0)
        score(14, 1)
        quantize_stage(15 + K_LAG, E_BLOCKS, E_BLOCKS + 1)
        quantize_stage(15 + K_LAG, E_BLOCKS + 1, BLOCKS)
        score(15, 0)
        score(15, 1)
        store_y(5, 2)
        store_scales(0, G - 1, [nc.sync])

        for half in range(2):
            round_y(6, half)
        for half in range(2):
            quantize_y(6, (half, half + 1))
        store_codes(6)
        for b in range(PACK):
            turn_y(6, b)
        for pair in (14, 15):
            weigh(pair, 0)
            weigh(pair, 1)
        store_y(6, 0)
        store_y(6, 2)
        for half in range(2):
            round_y(7, half)
        for half in range(2):
            quantize_y(7, (half, half + 1))
        for b in range(PACK - 1):
            turn_y(7, b)
        turn_y(7, PACK - 1, nc.vector.tensor_copy)
        store_y(7, 0)
        store_codes(7)
        store_scales(G - 1, G, [nc.sync])
        store_y(7, 2, 1)
        store_y(7, 3, 1)
